import numpy as np, ml_dtypes
CORES = [66,74,82,90,194,202,210,218]
N = 8
BF = ml_dtypes.bfloat16
def gentries(a):
    return np.ascontiguousarray(a.reshape(8, 16, -1).transpose(0, 2, 1)).reshape(8, -1)
def gtable(e):
    e = np.asarray(e); return np.ascontiguousarray(e.reshape(8, -1, 16).transpose(0, 2, 1)).reshape(128, -1).astype(np.int32)
C, L, M, P, CAP, S, Q, RING = 64, 4096, 16, 512, 48, 2, 2, False
Z = 63 * S
def media(rng):
    return rng.integers(0, M, (N, 8, L)), rng.integers(-63, 64, (N, 8, 128 * M))
def zones(rng):
    t = rng.integers(CAP // 2, CAP + 1, (N, 8)); zr = rng.integers(0, t + 1)
    return np.roll(t - zr, 1, axis=0), zr, P - t - np.roll(t, 1, axis=0)
def crowd(rng, zl, zr, ni, near):
    n = zl + zr + ni; x = rng.integers(0, L, (N, 8, P))
    for r in range(N):
        for g in range(8):
            a = (near * rng.random(zl[r, g]) ** 2).astype(np.int64); b = L - 1 - (near * rng.random(zr[r, g]) ** 2).astype(np.int64)
            x[r, g, :n[r, g]] = rng.permutation(np.concatenate([a, b, rng.integers(Z, L - Z, ni[r, g])]))
    return x, n
def names(rng):
    return rng.integers(1, 2 ** 20, (N, 8, P)) * rng.choice(np.array([-1, 1]), (N, 8, P))
def pack(x, v, w, n, med, kick):
    d = {"x": np.stack([gtable(a) for a in x]), "v": np.stack([gtable(a) for a in v]), "w": np.stack([gtable(a) for a in w])}
    d["live"] = np.repeat(n, 16, axis=1)[:, :, None].astype(np.int32); d["med"] = med.astype(np.int32); d["kick"] = kick.astype(np.int32); return d
def plain(rng):
    zl, zr, room = zones(rng); x, n = crowd(rng, zl, zr, rng.integers(room // 3, room + 1), Z)
    return x, rng.integers(-63, 64, (N, 8, P)), names(rng), n
def setup_inputs(rng):
    return pack(*plain(rng), *media(rng))
def setup_inputs_full(rng):
    s = rng.permutation(np.array([1, 1, 1, 1, -1, -1, -1, -1])); right = np.where(s > 0, CAP, 0); left = CAP - right
    zr = np.tile(right, (N, 1)); zl = np.tile(left, (N, 1))
    if not RING:
        zr[N - 1] = 0; zl[0] = 0
    ni = P - zl - zr
    if not RING:
        ni[N - 1] -= right; ni[0] -= left
    x, n = crowd(rng, zl, zr, ni, 63); med, kick = media(rng); b = 63 * (S + 1)
    med[:, :, :b] = M - 1; med[:, :, L - b:] = M - 1
    for g in range(8):
        kick[:, g, 128 * (M - 1):] = 63 * s[g]
    return pack(x, rng.integers(-63, 64, (N, 8, P)), names(rng), n, med, kick)
def setup_inputs_both(rng):
    zl = np.full((N, 8), CAP); zr = np.full((N, 8), CAP)
    if not RING:
        zl[0] = 0; zr[N - 1] = 0
    x, n = crowd(rng, zl, zr, P - zl - zr, 63); med, kick = media(rng); b = 63 * (S + 1); e = 128 * (M - 1)
    med[:, :, :b] = M - 1; med[:, :, L - b:] = M - 1; kick[:, :, e:e + 64] = -63; kick[:, :, e + 64:] = 63
    side = np.where(x < 63, -1, np.where(x >= L - 63, 1, 0)); v = np.where(side == 0, rng.integers(-63, 64, x.shape), 63 * side); w = np.abs(names(rng))
    for r in range(N):
        for g in range(8):
            for s in (-1, 0, 1):
                k = np.flatnonzero(side[r, g] == s); w[r, g, k] = w[r, g, k] * rng.permutation(1 - 2 * (np.arange(k.size) & 1))
    return pack(x, v, w, n, med, kick)
def setup_inputs_empty(rng):
    x, v, w, n = plain(rng); o = rng.permutation(8); keep = rng.random((N, 8)) > 0.4; keep[:, o[2]] = True; n = np.where(keep, n, 0)
    n[:, o[:2]] = 0; n[rng.integers(0, N), o[0]] = 1
    return pack(x, v, w, n, *media(rng))
def setup_inputs_edges(rng):
    x, v, w, n = plain(rng); med, kick = media(rng); far = (x >= Z) & (x < L - Z)
    y = (x & -64) + 63 * rng.integers(0, 2, x.shape); x = np.where(far & (y >= Z) & (y < L - Z), y, x)
    x = np.where(far, x, np.where(x < Z, rng.choice(np.array([0, 0, 1, 62, 63, 64]), x.shape), L - 1 - rng.choice(np.array([0, 0, 1, 62, 63, 64]), x.shape)))
    v = rng.choice(np.array([-63, -1, 0, 1, 63]), v.shape); kick = np.where(rng.random(kick.shape) < 0.75, rng.choice(np.array([-63, -62, -1, 0, 1, 62, 63]), kick.shape), kick)
    s = rng.permutation(np.array([1, 1, 1, -1, -1, -1, 0, 0]))[None, :, None]; w = np.where(s == 0, w, np.abs(w) * s)
    return pack(x, v, w, n, med, kick)
def setup_inputs_spread(rng):
    zl, zr, room = zones(rng); x, n = crowd(rng, zl, zr, np.maximum(1, (room * rng.random((N, 8)) ** 4).astype(np.int64)), Z)
    w = np.minimum(np.exp2(20 * rng.random((N, 8, P))).astype(np.int64), 2 ** 20 - 1) * rng.choice(np.array([-1, 1]), (N, 8, P))
    v = np.rint(63 * (2 * rng.random((N, 8, P)) - 1) ** 5).astype(np.int64)
    med = np.repeat((M * rng.random((N, 8, L // 16)) ** 3).astype(np.int64), 16, axis=2); kick = np.rint(63 * (2 * rng.random((N, 8, 128 * M)) - 1) ** 3).astype(np.int64)
    return pack(x, v, w, n, med, kick)
def run(x, v, w, n, med, kick):
    worst, most = 0, int(n.max()); ri, gi = np.arange(N)[:, None, None], np.arange(8)[None, :, None]; sh = np.array([[L], [0], [0]])
    for s in range(S):
        on = np.arange(P) < n[:, :, None]; c = x >> 6
        ch = np.zeros((N, 8, C), np.int64); np.add.at(ch, (ri, gi, c), np.where(on, np.sign(w), 0))
        E = np.add.accumulate(ch.transpose(1, 0, 2).reshape(8, N * C), axis=1).reshape(8, N, C).transpose(1, 0, 2)
        u = np.clip(v + np.take_along_axis(E, c, axis=2), -63, 63)
        for i in range(Q):
            m = np.take_along_axis(med, (x + u) & (L - 1), axis=2); u = np.take_along_axis(kick, 128 * m + 64 + u, axis=2)
        x = x + u; v = u
        if not RING:
            k = x[0] < 0; x[0] = np.where(k, -1 - x[0], x[0]); v[0] = np.where(k, -v[0], v[0])
            k = x[N - 1] >= L; x[N - 1] = np.where(k, 2 * L - 1 - x[N - 1], x[N - 1]); v[N - 1] = np.where(k, -v[N - 1], v[N - 1])
        lf, rt = on & (x < 0), on & (x >= L); st = on & ~lf & ~rt
        worst = max(worst, int(np.sum(lf, axis=2).max()), int(np.sum(rt, axis=2).max()))
        t = np.stack([x, v, w]); new = np.zeros((3, N, 8, P), np.int64); cnt = np.zeros((N, 8), np.int64)
        for r in range(N):
            a, b = (r + N - 1) % N, (r + 1) % N
            for g in range(8):
                e = np.concatenate([t[:, r, g][:, st[r, g]], t[:, a, g][:, rt[a, g]] - sh, t[:, b, g][:, lf[b, g]] + sh], axis=1)
                most = max(most, e.shape[1]); cnt[r, g] = min(e.shape[1], P); new[:, r, g, :cnt[r, g]] = e[:, :P]
        x, v, w = new; n = cnt
    return x, v, w, worst, most
def state(x, v, w, live, med, kick):
    h = [np.stack([gentries(a) for a in z]).astype(np.int64) for z in (x, v, w)]
    return h + [live[:, ::16, 0].astype(np.int64), med.astype(np.int64), kick.astype(np.int64)]
def check_inputs(d):
    big = 2 ** 20 - 1
    bad = [k for k, lo, hi in (("x", 0, L - 1), ("v", -63, 63), ("w", -big, big), ("live", 0, P), ("med", 0, M - 1), ("kick", -63, 63)) if d[k].min() < lo or d[k].max() > hi]
    if (d["w"] == 0).any():
        bad.append("w")
    if (d["live"].reshape(N, 8, 16) != d["live"].reshape(N, 8, 16)[:, :, :1]).any():
        bad.append("live")
    if bad:
        return bad
    worst, most = run(*state(d["x"], d["v"], d["w"], d["live"], d["med"], d["kick"]))[3:]
    return (["leavers"] if worst > CAP else []) + (["places"] if most > P else [])
def reference(x, v, w, live, med, kick):
    xe, ve, we, worst, most = run(*state(x, v, w, live, med, kick))
    return {"yx": np.stack([gtable(a) for a in xe]).astype(np.float32), "yv": np.stack([gtable(a) for a in ve]).astype(np.float32), "yw": np.stack([gtable(a) for a in we]).astype(np.float32)}

from concourse.bass import DstId, RemoteDMATransfer
from concourse.mybir import AluOpType as OP, ActivationFunctionType as AF

F, H, I, U = "float32", "bfloat16", "int32", "uint16"
BIG = float(2 ** 40)
B2A, B2B = 672, 1888
TURNS = "o" * 8 + "nonon" + "onnnnno" + "onononnnno" + "nnonnonnonnonnoo"
SCRATCH = {n: ("sbuf", [128, c], d) for n, c, d in [
    ("xi", 32, I), ("vi", 32, I), ("wi", 32, I), ("li", 4, I), ("medi", 256, I), ("kicki", 128, I), ("wp", 512, I),
    ("medb", 256, H), ("kickb", 128, H), ("medR", 4224, H), ("kickR", 2048, H), ("sel", 2048, H),
    ("ip", 4, I), ("cb", 32, F), ("c16", 32, F), ("kk", 128, H), ("cc", 72, F), ("ccm", 72, F), ("jq", 32, F), ("jl", 32, F),
    ("ones", 128, H), ("nones", 128, H), ("m1", 128, H), ("onesB", 128, H), ("onesF", 128, F), ("r0F", 128, F), ("r1F", 128, F),
    ("mk", 16, F), ("pa16", 16, F), ("pb16", 16, F), ("pat16", 16, F), ("pat", 608, H), ("opat", 40, U), ("operm", 32, U),
    ("ha", 72, F), ("hb", 72, F), ("hc", 72, F), ("hd", 72, F), ("ht", 432, F), ("junk", 512, H), ("acc", 4, F), ("rhs", 32, F),
    ("et", 72, I), ("eh", 32, F), ("ef", 72, F), ("sg", 32, F), ("al", 32, F), ("q", 32, F), ("one", 48, F), ("part", 32, H),
    ("t0", 40, F), ("t1", 40, F), ("t2", 40, F), ("t3", 40, F), ("t4", 40, F), ("t5", 40, F), ("land1", 8, H), ("t6", 40, F),
    ("xB", 40, F), ("x2B", 40, F), ("xqB", 32, F), ("vB", 32, F), ("a0", 40, F), ("a1", 40, F), ("uB", 40, F), ("m63", 40, F),
    ("oh", 32, U), ("oc", 32, U), ("oa", 40, U), ("ob", 40, U), ("od", 40, U), ("of", 32, U), ("thr", 40, F), ("thl", 40, F),
    ("we", 512, F), ("te", 512, F), ("wm", 608, H), ("tm", 608, H), ("tk", 608, H), ("uw", 608, F),
    ("base", 512, F), ("base2", 608, F), ("dw", 512, F), ("idf", 128, F), ("onef", 128, F),
    ("xp", 32, F), ("f1", 80, H), ("f2", 80, H), ("s1", 80, H), ("d1", 80, H), ("d2", 80, H), ("wn", 40, F), ("g1", 40, F), ("g2", 40, F),
    ("it", 120, F), ("it2", 120, F), ("d3", 120, F), ("djn", 32, F), ("k2", 40, F), ("k3", 40, F), ("d0n", 40, F), ("fq", 32, H),
    ("al2", 40, H), ("sa", 40, H), ("shB", 8, F), ("tu", 96, F), ("tx", 96, F), ("junk2", 32, F),
    ("win1", B2A + 48, F), ("win2", B2B + 48, F), ("land2", 96, F), ("fin", 616, F), ("fo", 512, F),
    ("out2", 4, F), ("in2", 4, F), ("out3", 4, F), ("in3", 4, F),
]}
SCRATCH.update({"pa": ("psum", [128, 1024], F), "pb": ("psum", [128, 1024], F), "pc": ("psum", [128, 1024], F),
                "pd": ("psum", [128, 512], F), "pe": ("psum", [128, 512], F)})
SEMAPHORES = (["ev", "es", "et", "eg", "loc", "a2l", "a2r", "a3l", "a3r", "c2", "c3"] + ["r%d" % k for k in range(7)]
              + ["d%d" % k for k in range(11)])


def rank_program(g, core, T, topo):
    rank = T.rank_of(core)
    if rank is None:
        return
    N = len(T.cores)
    hasL, hasR = rank > 0, rank < N - 1
    end = not (hasL and hasR)
    Q = {"v": g.vector, "s": g.scalar, "t": g.tensor, "g": g, "y": g.sync}
    cnt = {}
    seen = {k: {} for k in Q}
    hist = {}
    nd = [0]

    def A(name, lo=0, hi=None, st=1):
        hi = SCRATCH[name][1][1] if hi is None else hi
        return (T[name][:, lo:hi:st] if st > 1 else T[name][:, lo:hi], [(name, lo, hi)])

    def C(k):
        return A("cb", k, k + 1)

    def IND(win, off):
        return (win[0].indirect(off[0]), win[1], off[1])

    def wait(q, sem, val, clock):
        if seen[q].get(sem, 0) >= val:
            return
        Q[q].wait_ge(T.sem[sem], val)
        seen[q][sem] = val
        for k, x in clock.items():
            if seen[q].get(k, 0) < x:
                seen[q][k] = x

    def order(q, rd, wr):
        need = {}
        for keys, w in ((rd, False), (wr, True)):
            for (n, lo, hi) in keys:
                ps = SCRATCH[n][0] == "psum"
                for (l2, h2, w2, sem, val, ck) in hist.get(n, []):
                    if ps and q == "t" and sem == "et":
                        continue
                    if (ps and sem != "e" + q) or ((w or w2) and l2 < hi and lo < h2):
                        if need.get(sem, (0, None))[0] < val:
                            need[sem] = (val, ck)
        for sem, (val, ck) in sorted(need.items(), key=lambda z: -len(z[1][1])):
            wait(q, sem, val, ck)

    def note(q, rd, wr, sem, val):
        ck = dict(seen[q])
        for keys, w in ((rd, False), (wr, True)):
            for (n, lo, hi) in keys:
                hist.setdefault(n, []).append((lo, hi, w, sem, val, ck))

    def run(q, fn, out, ins, more=()):
        rd, wr = [], list(out[1]) + [k for m in more for k in m[1]]
        if len(out) > 2:
            rd += out[2]
        for a in ins:
            if isinstance(a, tuple):
                rd += a[1] + (a[2] if len(a) > 2 else [])
        order(q, rd, wr)
        sem = "e" + q
        cnt[sem] = cnt.get(sem, 0) + 1
        fn().then_inc(T.sem[sem], 1)
        note(q, rd, wr, sem, cnt[sem])

    def ap(a):
        return a[0] if isinstance(a, tuple) else a

    def ts(out, a, s1, o1, s2=None, o2=None):
        if o2 is None:
            run("v", lambda: g.vector.tensor_scalar(out[0], a[0], ap(s1), None, o1), out, [a, s1])
        else:
            run("v", lambda: g.vector.tensor_scalar(out[0], a[0], ap(s1), ap(s2), o1, o2), out, [a, s1, s2])

    def tt(out, a, b, o):
        run("v", lambda: g.vector.tensor_tensor(out[0], a[0], b[0], o), out, [a, b])

    def cp(out, a):
        run("v", lambda: g.vector.tensor_copy(out[0], a[0]), out, [a])

    def ms(out, c):
        run("v", lambda: g.vector.memset(out[0], c), out, [])

    def scan(out, d0, d1):
        run("v", lambda: g.vector.tensor_tensor_scan(out[0], d0[0], d1[0], 0.0, OP.mult, OP.add), out, [d0, d1])

    def act(out, a, scale=1.0, bias=0.0, fn=AF.Identity, acc=None):
        if acc is None:
            run("s", lambda: g.scalar.activation(out[0], a[0], fn, bias=ap(bias), scale=ap(scale)), out, [a, scale, bias])
        else:
            run("s", lambda: g.scalar.activation(out[0], a[0], fn, accum_out=acc[0]), out, [a], [acc])

    def mm(out, l, r, start=True, stop=True):
        run("t", lambda: g.tensor.matmul(out[0], l[0], r[0], start, stop), out, [l, r])

    def iota(out, pat, cm=0, b=0):
        if SCRATCH[out[1][0][0]][2] != I:
            run("g", lambda: g.iota(out[0], pat, b, cm, allow_small_or_imprecise_dtypes=True), out, [])
        else:
            run("g", lambda: g.iota(out[0], pat, b, cm), out, [])

    def dma(q, out, src, rd=(), wr=()):
        order(q, list(rd), list(wr))
        sem = "d%d" % nd[0]
        nd[0] += 1
        cnt[sem] = 16
        Q[q].dma_start(out, src).then_inc(T.sem[sem], 16)
        note(q, list(rd), list(wr), sem, 16)

    def arrives(a, sem, n):
        cnt[sem] = n
        for (nm, lo, hi) in a[1]:
            hist.setdefault(nm, []).append((lo, hi, True, sem, n, {}))

    def bits(es):
        return sum(1 << e for e in es)

    def dst(r):
        rid, pid = topo.addr(T.cores[r], core)
        return DstId(rid=rid, pnc=pid)

    def engines_to(s, ds):
        return [e for e in topo.engines(T.cores[s], T.cores[ds[0]]) if all(e in topo.engines(T.cores[s], T.cores[d]) for d in ds)]

    def shares(s):
        nb = [d for d in (s - 1, s + 1) if 0 <= d < N]
        es = engines_to(s, nb)
        k = len(es) // len(nb)
        return {d: es[j * k:(j + 1) * k] for j, d in enumerate(nb)}

    def send(trs, srcs, n):
        order("g", [k for a in srcs for k in a[1]], [])
        g.remote_dma_fused(trs, local_sem=T.sem.loc)
        cnt["loc"] = cnt.get("loc", 0) + n

    def exchange(win, b2, land, lo, semL, semR):
        sh, trs, srcs = shares(rank), [], []
        if hasR:
            a = A(win, 0, 48)
            trs.append(RemoteDMATransfer(dst_ids=[dst(rank + 1)], dma_engine_mask=bits(sh[rank + 1]), remote_sem=T.sem[semL],
                                         src=a[0], dst=T[land][:, lo:lo + 48]))
            srcs.append(a)
        if hasL:
            a = A(win, b2, 48 + b2)
            trs.append(RemoteDMATransfer(dst_ids=[dst(rank - 1)], dma_engine_mask=bits(sh[rank - 1]), remote_sem=T.sem[semR],
                                         src=a[0], dst=T[land][:, lo + 48:lo + 96]))
            srcs.append(a)
        send(trs, srcs, sum(len(x) for x in sh.values()))
        if hasL:
            arrives(A(land, lo, lo + 48), semL, len(shares(rank - 1)[rank]))
        if hasR:
            arrives(A(land, lo + 48, lo + 96), semR, len(shares(rank + 1)[rank]))

    def ahead(out, land, sem, d, n):
        if 0 <= rank + d < N:
            es = engines_to(rank, [rank + d])
            a = A(out, 0, n)
            send([RemoteDMATransfer(dst_ids=[dst(rank + d)], dma_engine_mask=bits(es), remote_sem=T.sem[sem],
                                    src=a[0], dst=T[land][:, 0:n])], [a], len(es))
        if 0 <= rank - d < N:
            arrives(A(land, 0, n), sem, len(engines_to(rank - d, [rank])))

    PM, BC, SI, SI64, B127, B64, LF, PM1, PM32, PM16, SC1, BI1, SC2, BI2, SHL, SHR, PRE, NAL, NSN, K5, MS, MB, RS, RB, B4160, IS15 = range(26)
    mk = lambda r: A("mk", r, r + 1)
    sel = lambda i: A("sel", 128 * i, 128 * i + 128)

    dma("y", T.wi[:], T.w[:], wr=A("wi")[1])
    dma("s", T.li[:, 0:1], T.live[:], wr=A("li")[1])
    dma("y", T.medi[:], T.med[:], wr=A("medi")[1])
    dma("s", T.xi[:], T.x[:], wr=A("xi")[1])
    dma("y", T.kicki[:], T.kick[:], wr=A("kicki")[1])
    dma("s", T.vi[:], T.v[:], wr=A("vi")[1])

    iota(A("ip", 0, 1), [[0, 1]], 1)
    iota(A("kk"), [[-16, 8], [0, 16]], 1)
    iota(A("c16"), [[16, 32]])
    iota(A("cc"), [[1, 72]])
    iota(A("ht", 72, 144), [[0, 72]])
    iota(A("ht", 288, 360), [[0, 72]])
    ms(A("one"), 1.0)
    ts(A("ip", 1, 2), A("ip", 0, 1), 15, OP.bitwise_and)
    ms(A("et"), 0)
    cp(C(PM), A("ip", 1, 2))
    ts(sel(0), A("kk"), 0.0, OP.is_equal)
    ts(C(IS15), C(PM), 15.0, OP.not_equal, BIG, OP.mult)
    ts(C(SI), C(PM), 15.0, OP.is_equal, 1.0 / BIG, OP.max)
    ts(A("ones"), A("kk"), C(PM), OP.is_equal)
    ts(C(BC), C(IS15), 1.0, OP.max)
    act(C(PM1), C(PM), 1.0, 1.0)
    act(C(SI64), C(SI), 1.0 / 64)
    act(A("onesF"), A("ones"))
    act(A("onesB"), A("ones"), BIG)
    act(C(B127), C(BC), 127.0)
    act(C(PM32), C(PM), 32.0)
    act(A("nones"), A("ones"), -1.0)
    act(A("onesB", 15, 128, 16), A("ones", 15, 128, 16))
    for i in range(1, 4):
        ts(sel(i), A("kk"), float(i), OP.is_equal)
    ts(A("jl"), A("c16"), C(PM), OP.add)
    ts(A("mk"), A("cc", 0, 16), C(PM), OP.is_equal)
    ts(A("pa16"), A("cc", 0, 16), C(PM), OP.not_equal)
    ts(A("pb16"), A("cc", 0, 16), C(PM1), OP.is_equal, BIG, OP.mult)
    ts(A("opat", 0, 38), A("one", 0, 38), C(PM), OP.mult)
    ts(A("ccm"), A("cc"), 64.0 if not hasR else 99.0, OP.min, 0.25, OP.mult)
    tt(A("pat16"), A("pa16"), A("pb16"), OP.max)
    act(A("pat"), IND(A("pat16"), A("opat", 0, 38)))
    for i in range(4, 8):
        ts(sel(i), A("kk"), float(i), OP.is_equal)

    cp(C(LF), A("li", 0, 1))
    ts(A("sg"), A("wi"), -1.0, OP.max, 1.0, OP.min)
    ts(A("al"), A("jl"), C(LF), OP.is_lt)
    ts(A("ccm"), A("ccm"), C(PM), OP.subtract)
    tt(A("q"), A("sg"), A("al"), OP.mult)
    ts(A("t0", 0, 32), A("xi"), -2048.0, OP.add)
    if hasR:
        scan(A("part"), A("one", 0, 32), A("q"))
        ds = list(range(N - 1, rank, -1))
        es = engines_to(rank, ds)
        a = A("part", 31, 32)
        send([RemoteDMATransfer(dst_ids=[dst(d) for d in ds], dma_engine_mask=bits(es), remote_sem=T.sem["r%d" % rank],
                                srcs=[a[0]], dsts=[T.land1[:, rank:rank + 1] for d in ds])], [a], len(es))
    for s in range(rank):
        arrives(A("land1", s, s + 1), "r%d" % s, len(engines_to(s, list(range(s + 1, N)))))

    def rep_med(k, p):
        for i in range(4):
            mm(A(p, 256 * i, 256 * i + 256), sel(4 * k + i), A("medb"))

    def rep_kick(k, p):
        for i in range(8):
            mm(A(p, 128 * i, 128 * i + 128), sel(8 * k + i), A("kickb"))

    def count_cells():
        for s in range(2):
            act(A("junk"), IND(A("ht", 216 * s, 216 * s + 216), A("oh")), acc=A("acc", s, s + 1))

    def gather(out, win, off, c0, m, c1):
        if m < c1:
            act(A(out, 16 * m, 16 * c1), IND(A(win), A(off, m, c1)))
        cp(A(out, 16 * c0, 16 * m), IND(A(win), A(off, c0, m)))

    medc = lambda k: A("medR", 64 + 1024 * k, 1088 + 1024 * k)
    ts(A("t1", 0, 32), A("q"), -4608.0, OP.mult, 4608.0, OP.add)
    tt(A("t2", 0, 32), A("t0", 0, 32), A("al"), OP.mult)
    ts(A("ha"), A("ccm"), 0.25, OP.is_le)
    ts(A("hb"), A("ccm"), 0.5, OP.is_le, 2048.0, OP.mult)
    ts(A("medb"), A("medi"), 128.0, OP.mult)
    ts(A("t3", 0, 32), A("t1", 0, 32), C(BC), OP.mult)
    ts(A("xB", 0, 32), A("t2", 0, 32), 2048.0, OP.add, C(BC), OP.mult)
    tt(A("ht", 0, 72), A("ha"), A("hb"), OP.add)
    tt(A("xqB"), A("xB", 0, 32), A("t3", 0, 32), OP.add)
    ts(A("ht", 144, 216), A("ht", 0, 72), -1.0, OP.mult)
    ts(A("oh"), A("xqB"), C(SI64), OP.mult, 32.5 / 64, OP.add)
    ts(A("hc"), A("ccm"), 0.75, OP.is_le)
    ts(A("hd"), A("ccm"), 1.0, OP.is_le, 2048.0, OP.mult)
    ts(sel(8), A("kk"), 8.0, OP.is_equal)
    tt(A("ht", 216, 288), A("hc"), A("hd"), OP.add)
    ts(sel(9), A("kk"), 9.0, OP.is_equal)
    ts(A("ht", 360, 432), A("ht", 216, 288), -1.0, OP.mult)
    for i in range(10, 16):
        ts(sel(i), A("kk"), float(i), OP.is_equal)
    ts(A("kickb"), A("kicki"), 64.0, OP.add)
    rep_med(0, "pa")
    rep_med(1, "pb")
    rep_med(2, "pc")
    count_cells()
    ts(A("oc"), A("xB", 0, 32), C(SI64), OP.mult, 32.5 / 64, OP.add)
    cp(medc(0), A("pa"))
    for s in range(2):
        ts(A("rhs", s, 32, 2), A("mk"), A("acc", s, s + 1), OP.mult)
    mm(A("pe", 0, 32), A("onesF"), A("rhs"))
    rep_med(3, "pa")
    act(medc(1), A("pb"))
    rep_kick(0, "pb")
    act(medc(2), A("pc"))
    rep_kick(1, "pc")
    cp(A("medR", 4160, 4224), A("medR", 64, 128))
    ts(A("vB"), A("vi"), 64.0, OP.add, C(BC), OP.mult)
    ts(A("operm"), A("cc", 0, 32), C(PM32), OP.add)
    ts(A("et", 2, 66, 2), A("pe", 0, 32), 1.0 / 2048, OP.mult)
    ts(A("eh"), A("et", 2, 66, 2), -2048.0, OP.mult)
    tt(A("et", 1, 65, 2), A("pe", 0, 32), A("eh"), OP.add)
    gather("we", "et", "oc", 0, 32, 32)
    scan(A("te"), A("pat", 0, 512), A("we"))
    tt(A("a0", 0, 32), A("te", 15, 512, 16), A("vB"), OP.add)
    cp(medc(3), A("pa"))
    cp(A("medR", 0, 64), A("medR", 4096, 4160))
    act(A("kickR", 0, 1024), A("pb"))
    act(A("kickR", 1024, 2048), A("pc"))

    iota(A("wp"), [[0, 512]])
    dma("y", T.wp[0::16, :], T.x[:], wr=[("wp", 0, 256)])
    dma("y", T.wp[2::16, :], T.w[:], wr=[("wp", 256, 512)])
    run("g", lambda: g.affine_select(T.m1[:], T.nones[:], [[-1, 128]], OP.is_ge, 0.0, 0, 1), A("m1"), [A("nones")])
    for f, d, nc, b2 in (("f1", "d1", 32, B2A), ("f2", "d2", 38, B2B)):
        if not hasR:
            iota(A(f, 0, nc), [[0, nc]])
        if not hasL:
            iota(A(f, nc + 1, 2 * nc + 1), [[0, nc]])
        iota(A(f, nc, nc + 1), [[0, 1]], 0, b2 // 16)
        iota(A(d, 0, 2 * nc + 1), [[0, 2 * nc + 1]], 0, 1)
        iota(A(d, nc, nc + 1), [[0, 1]])
    iota(A("onef"), [[0, 128]], 0, 1)
    run("g", lambda: g.affine_select(T.idf[:], T.onef[:], [[-1, 128]], OP.is_equal, 0.0, 0, 1), A("idf"), [A("onef")])
    iota(A("d3", 0, 114), [[0, 114]], 0, 1)
    iota(A("d3", 0, 114, 3), [[0, 38]])
    if end:
        iota(A("it", 0, 96), [[0, 96]])
    iota(A("djn"), [[-16, 32]], -1, -48)
    iota(A("win2", 0, 560), [[0, 560]])
    iota(A("fin", 608, 616), [[0, 8]])
    iota(A("jq"), [[1, 16], [256, 2]])
    iota(A("k2", 0, 38), [[-16, 38]], -1, 48 - 1168)
    iota(A("k3", 0, 38), [[-16, 38]], -1, -1168 - (B2B if hasL else 0))
    if hasR:
        iota(A("m63", 32, 35), [[0, 3]])
    if not hasL:
        iota(A("land2", 0, 48), [[0, 48]])
        iota(A("fin", 512, 560), [[0, 48]])
    if not hasR:
        iota(A("land2", 48, 96), [[0, 48]])
        iota(A("fin", 560, 608), [[0, 48]])

    if hasL:
        for s in range(rank - 1, -1, -1):
            mm(A("pd", 0, 1), A("onesB"), A("land1", s, s + 1), s == rank - 1, s == 0)
        ts(A("a1", 0, 32), A("a0", 0, 32), A("pd", 0, 1), OP.add, C(BC), OP.max)
        ts(A("uB", 0, 32), A("a1", 0, 32), C(B127), OP.min)
    else:
        ts(A("uB", 0, 32), A("a0", 0, 32), C(BC), OP.max, C(B127), OP.min)

    def scatterings(c0, c1, nv, xb, side=None):
        calls = []
        L = lambda n: A(n, c0, c1)
        W = lambda n: A(n, 16 * c0, 16 * c1)
        last = lambda n: A(n, 16 * c0 + 15, 16 * c1, 16)

        def level(k, a, b, t, off, win, res):
            def pick():
                gather("wm", win, off, c0, c0 + nv[k], c1)
                if side:
                    side(k)
            calls.extend([lambda: tt(L(t), a, b, OP.add), lambda: ts(L(off), L(t), C(SI), OP.mult, 0.25, OP.add), pick,
                          lambda: scan(W(res), W("pat"), W("wm"))])

        for k in range(2):
            u = last("tk") if k else L("uB")
            level(2 * k, u, L(xb), "t0", "oa", "medR", "tm")
            level(2 * k + 1, last("tm"), u, "t1", "ob", "kickR", "tk")
        return calls

    def move(step, nc, u, f, d, win, base):
        n = 16 * nc
        fr, fl, wn = A(f, 0, nc), A(f, nc + 1, 2 * nc + 1), A("wn", 0, nc)
        if step == 1:
            act(A("uw", 0, n), IND(A("kickR"), A("ob", 0, nc)), C(SC1), C(BI1))
        else:
            act(A("uw", 512, n), IND(A("kickR"), A("ob", 32, nc)), C(SC2), C(BI2))
        if hasR:
            tt(fr, u, A("thr", 0, nc), OP.is_ge)
        if hasL:
            tt(fl, u, A("thl", 0, nc), OP.is_lt)
        scan(A("s1", 0, 2 * nc + 1), A(d, 0, 2 * nc + 1), A(f, 0, 2 * nc + 1))
        mm(A("pa", 0, 2 * nc + 1), A("m1"), A(f, 0, 2 * nc + 1), True, False)
        mm(A("pa", 0, 2 * nc + 1), A("ones"), A("s1", 0, 2 * nc + 1), False, True)
        if step == 1:
            if hasL:
                tt(A("fq"), fl, A("q"), OP.mult)
                mm(A("pb", 0, 32), A("ones"), A("fq"))
                act(A("junk2"), A("pb", 0, 32), acc=A("out2", 0, 1))
            ahead("out2", "in2", "c2", -1, 1)
        w = fr if hasR else fl
        if not end:
            w = A("t3", 0, nc)
            tt(w, fl, fr, OP.add)
        if step == 1:
            tt(A("t2", 0, 32), u, A("xqB"), OP.add)
        elif end:
            tt(A("t4", 0, nc), u, A("thl" if hasR else "thr", 0, nc), OP.is_lt if hasR else OP.is_ge)
        ts(wn, w, -1.0, OP.add)
        if step == 1:
            ts(A("oh"), A("t2", 0, 32), C(SI64), OP.mult, -31.5 / 64, OP.add)
            count_cells()
            for s in range(2):
                act(A("rhs", s, 32, 2), A("mk"), A("acc", s, s + 1))
            mm(A("pe", 0, 32), A("onesF"), A("rhs"))
            mm(A("pb", 512, 1024), A("idf"), A("uw", 0, 512), False, True)
        else:
            mm(A("pb", 0, 2), A("ones"), A("s1", nc - 1, 2 * nc + 1, nc + 1))
            if hasR:
                act(A("out3", 0, 1), A("pb", 0, 1))
                act(A("out3", 1, 2), A("pb", 0, 1), -1.0, 48.0)
            ahead("out3", "in3", "c3", 1, 2)
            if end:
                ts(A("it", 1 if hasR else 0, 3 * nc, 3), A("t4", 0, nc), 512.0, OP.mult)
            if hasR:
                tt(A("g1", 0, nc), fr, wn, OP.add)
                fr = A("g1", 0, nc)
            if hasL:
                tt(A("g2", 0, nc), fl, wn, OP.add)
                fl = A("g2", 0, nc)
        tt(A("it", 2, 3 * nc, 3), wn, A("djn") if step == 1 else A("d0n", 0, nc), OP.mult)
        if hasR:
            tt(A("it", 0, 3 * nc, 3), A("pa", 0, nc), fr, OP.mult)
        if hasL:
            tt(A("it", 1, 3 * nc, 3), A("pa", nc + 1, 2 * nc + 1), fl, OP.mult)
        scan(A("it2", 0, 3 * nc), A("d3", 0, 3 * nc), A("it", 0, 3 * nc))
        cp(A("od", 0, nc), A("it2", 2, 3 * nc, 3))
        tt(IND(A(win), A("od", 0, nc)), A("uw", 0, n), A(base, 0, n), OP.add)

    def limits(xb, c0, c1):
        act(A("thr", c0, c1), A(xb, c0, c1), -1.0, C(B4160))
        act(A("thl", c0, c1), A(xb, c0, c1), -1.0, C(B64))

    def side1(k):
        if k == 0:
            if hasL:
                ts(C(PRE), A("pd", 0, 1), C(SI), OP.mult)
            else:
                ms(C(PRE), 0.0)
            ts(A("win1", 0, 48), A("one"), mk(0), OP.mult, 6144.0, OP.mult)
            act(A("base", 0, 256), IND(A("wp"), A("operm", 0, 16)))
        if k == 1:
            ts(A("win1", B2A, 48 + B2A), A("one"), mk(0), OP.mult, -2048.0, OP.mult)
            ts(A("win2", B2B, 48 + B2B), A("one"), mk(0), OP.mult, -4096.0, OP.mult)
            act(A("base", 256, 512), IND(A("wp"), A("operm", 16, 32)))
            mm(A("pb", 512, 1024), A("idf"), A("base"), True, False)
        if k == 2:
            ts(A("shB", 0, 3), A("one", 0, 3), C(BC), OP.mult, -4096.0 if hasL else 2048.0, OP.mult)
            ts(A("shB", 3, 6), A("one", 0, 3), C(BC), OP.mult, 4096.0 if hasR else 2048.0, OP.mult)
            act(C(B4160), C(BC), 4160.0)
            act(C(B64), C(BC), 64.0)
            act(C(SC1), mk(0), 1.0, mk(1))
            act(C(BI1), mk(0), -64.0)
            limits("xB", 0, 32)

    for call in scatterings(0, 32, (16, 16, 16, 18), "xB", side1):
        call()
    u = A("tk", 15, 512, 16)
    move(1, 32, u, "f1", "d1", "win1", "base")
    exchange("win1", B2A, "land2", 0, "a2l", "a2r")

    act(C(SC2), mk(0), 1.0, mk(3))
    act(A("r1F"), sel(1))
    act(A("r0F"), sel(0))
    act(A("m63", 35, 38), A("one", 0, 3), C(BC))
    act(C(SHL), mk(0), -4096.0)
    act(C(SHR), mk(0), 4096.0)
    tt(A("xp"), u, A("xB", 0, 32), OP.add)
    ts(A("et", 2, 66, 2), A("pe", 0, 32), 1.0 / 2048, OP.mult)
    ts(A("oc"), A("xp"), C(SI64), OP.mult, -31.5 / 64, OP.add)
    ts(A("eh"), A("et", 2, 66, 2), -2048.0, OP.mult)
    ts(A("t0", 0, 32), A("xp"), C(SI), OP.mult, -2112.0, OP.add)
    tt(A("et", 1, 65, 2), A("pe", 0, 32), A("eh"), OP.add)
    tt(A("t1", 0, 32), A("al"), A("wn", 0, 32), OP.mult)
    if not hasL:
        cp(A("et", 0, 1), A("et", 1, 2))
    if not hasR:
        cp(A("et", 65, 66), A("et", 64, 65))
    ts(A("ef"), A("et"), C(PRE), OP.add)
    gather("wm", "ef", "oc", 0, 14, 32)
    xr, v2 = A("t0", 0, 32), u
    if end:
        ts(A("t2", 0, 32), xr, -1.0, OP.mult, -4097.0 if hasR else 4095.0, OP.add)
        ts(A("t4", 0, 32), xr, -2048.0 if hasR else 2048.0, OP.is_lt if hasR else OP.is_ge, C(BC), OP.mult)
        ts(A("t5", 0, 32), u, C(SI), OP.mult, -64.0, OP.add)
        tt(A("t3", 0, 32), xr, A("t2", 0, 32), OP.max if hasR else OP.min)
        tt(A("t6", 0, 32), A("t4", 0, 32), A("t5", 0, 32), OP.mult)
        ts(A("t5", 0, 32), A("t6", 0, 32), -2.0, OP.mult)
        tt(A("vB"), A("t5", 0, 32), u, OP.add)
        xr, v2 = A("t3", 0, 32), A("vB")
    tt(A("t2", 0, 32), xr, A("t1", 0, 32), OP.mult)
    ts(A("al2", 0, 32), A("t1", 0, 32), -1.0, OP.mult)
    scan(A("tm", 0, 512), A("pat", 0, 512), A("wm", 0, 512))
    act(A("t4", 0, 32), A("t2", 0, 32), -1.0, 2048.0)
    act(A("x2B", 0, 32), A("t4", 0, 32), C(BC))
    act(A("a0", 32, 35), A("m63", 35, 38), A("ef", 1, 2))
    act(A("a0", 35, 38), A("m63", 35, 38), A("ef", 64, 65))
    act(C(BI2), C(SC2), -64.0)
    act(C(PM16), C(PM), 16.0)
    if hasR:
        ts(A("m63", 0, 32), A("t2", 0, 32), -1984.0, OP.is_le, C(BC), OP.mult)
    tt(A("a0", 0, 32), A("tm", 15, 512, 16), v2, OP.add)
    av = "a1" if hasR else "a0"
    if hasR:
        ts(A("t5", 0, 38), A("m63", 0, 38), A("in2", 0, 1), OP.mult)
        tt(A("a1", 0, 38), A("a0", 0, 38), A("t5", 0, 38), OP.add)
    ts(A("uB", 0, 32), A(av, 0, 32), C(BC), OP.max, C(B127), OP.min)
    if end:
        edge = -1.0 if hasR else 8191.0
        act(C(RS), mk(0), -2.0 if hasR else 2.0)
        act(C(RB), mk(0), -abs(edge))
        act(C(MB), mk(0), edge)
        act(C(MS), C(SC2), -1.0, mk(2))

    def side2(k):
        if k == 0:
            limits("x2B", 0, 32)
            act(A("jq"), A("jq"), 1.0, C(PM16))
        if k == 1:
            act(A("dw") if end else A("base2", 0, 512), A("pb", 512, 1024))
        if k == 2 and end:
            act(A("pd", 0, 512), A("dw"), C(RS), C(RB), AF.Relu)
        if k == 3:
            act(A("uw", 0, 512), IND(A("kickR"), A("ob", 0, 32)), C(SC2), C(BI2))
            if end:
                act(A("win2", 560, 1072), A("win2", 48, 560), 1.0, C(MB))

    def spread():
        mm(A("pc", 0, 96), A("r1F"), A("land2"))
        mm(A("pe", 0, 96), A("r0F"), A("land2"))
        scan(A("tu"), A("pat", 0, 96), A("pc", 0, 96))

    def ranks():
        scan(A("sa", 0, 38), A("one", 0, 38), A("al2", 0, 38))
        mm(A("pb", 0, 38), A("m1"), A("al2", 0, 38), True, False)
        mm(A("pb", 0, 38), A("ones"), A("sa", 0, 38), False, True)
        mm(A("pb", 40, 41), A("ones"), A("sa", 37, 38))

    def rows():
        act(A("base2", 512, 560), A("land2", 0, 48), 1.0, C(SHL))
        act(A("base2", 560, 608), A("land2", 48, 96), 1.0, C(SHR))
        limits("x2B", 32, 38)
        act(C(NAL), A("pb", 40, 41), 1.0, float(B2B))

    new = [spread,
           lambda: tt(A(av, 32, 38), A(av, 32, 38), A("tu", 15, 96, 16), OP.add),
           lambda: scan(A("tx"), A("pat", 0, 96), A("pe", 0, 96)),
           lambda: ts(A("uB", 32, 38), A(av, 32, 38), C(BC), OP.max, C(B127), OP.min),
           lambda: tt(A("x2B", 32, 38), A("tx", 15, 96, 16), A("shB", 0, 6), OP.add)] + scatterings(32, 38, (6, 6, 6, 6), "x2B")
    own = scatterings(0, 32, (18, 18, 6, 6), "x2B", side2) + [
        lambda: ts(A("al2", 32, 38), A("tu", 15, 96, 16), C(SI), OP.mult, 0.5, OP.is_ge), ranks,
        lambda: tt(A("t2", 0, 38), A("pb", 0, 38), A("k2", 0, 38), OP.add), rows,
        lambda: tt(A("t3", 0, 38), A("t2", 0, 38), A("al2", 0, 38), OP.mult),
        lambda: tt(A("d0n", 0, 38), A("k3", 0, 38), A("t3", 0, 38), OP.subtract)]
    if end:
        own.append(lambda: tt(A("base2", 0, 512), A("dw"), A("pd", 0, 512), OP.add if hasR else OP.subtract))

    for ch in TURNS:
        calls = new if ch == "n" else own
        if calls:
            calls.pop(0)()
    for call in own + new:
        call()
    move(2, 38, A("tk", 15, 608, 16), "f2", "d2", "win2", "base2")
    exchange("win2", B2B, "fin", 512, "a3l", "a3r")

    if end:
        act(A("pc", 0, 512), A("win2", 560, 1072), C(MS), C(MB))
    else:
        act(A("fin", 0, 512), A("win2", 48, 560))
    ts(C(NSN), A("pb", 0, 1), A("pb", 1, 2), OP.add, C(NAL), OP.subtract)
    ts(A("t0", 0, 32), A("jq"), C(NSN), OP.add)
    ts(C(K5), C(NSN), 512.0 if hasL else 560.0, OP.add)
    ts(A("t1", 0, 32), A("t0", 0, 32), 0.0, OP.is_ge, C(K5), OP.mult)
    tt(A("t2", 0, 32), A("jq"), A("t1", 0, 32), OP.add)
    if end:
        tt(A("fin", 0, 512), A("win2", 48, 560), A("pc", 0, 512), OP.add)
    src = A("t2", 0, 32)
    if hasL:
        ts(A("t3", 0, 32), A("t0", 0, 32), A("in3", 0, 1), OP.is_ge, A("in3", 1, 2), OP.mult)
        tt(A("t4", 0, 32), src, A("t3", 0, 32), OP.add)
        src = A("t4", 0, 32)
    ts(A("of"), src, 608.0, OP.min)
    if hasL:
        ts(A("fin", 512, 560), A("fin", 512, 560), C(SHL), OP.add)
    if hasR and hasL:
        act(A("fin", 560, 608), A("fin", 560, 608), 1.0, C(SHR))
    elif hasR:
        ts(A("fin", 560, 608), A("fin", 560, 608), C(SHR), OP.add)
    gather("fo", "fin", "of", 0, 16, 32)
    dma("y", T.yx[:], T.fo[0::16, :], rd=A("fo")[1])
    dma("s", T.yv[:], T.fo[3::16, :], rd=A("fo")[1])
    dma("y", T.yw[:], T.fo[2::16, :], rd=A("fo")[1])
    for sem, n in cnt.items():
        if not any(seen[q].get(sem, 0) >= n for q in Q):
            wait("g" if sem == "loc" else "y", sem, n, {})
